import numpy as np
import ml_dtypes


def mxq(x, axis, fmt="e4m3"):
    dtype, down = {"e4m3": (ml_dtypes.float8_e4m3fn, 7), "e5m2": (ml_dtypes.float8_e5m2, 14)}[fmt]
    v = np.moveaxis(np.asarray(x, np.float32).astype(ml_dtypes.bfloat16).astype(np.float64), axis, -1)
    blocks = v.reshape(v.shape[:-1] + (-1, 32))
    amax = np.abs(blocks).max(-1, keepdims=True)
    byte = np.maximum(np.where(amax > 0, np.frexp(amax)[1] - 1 + 127, 0) - down, 1)
    scale = np.exp2(byte - 127.0)
    codes = (blocks / scale).astype(np.float32).astype(dtype).astype(np.float64)
    return np.moveaxis((codes * scale).reshape(v.shape), -1, axis)


WIDE = False


def mx_kscale(k):
    if not WIDE:
        return np.ones(k)
    levels = np.array([10, -10, 5, -5, 0])
    if k % 512:
        return np.exp2(np.random.permutation(np.resize(levels, k // 32))).repeat(32)
    a = np.empty((k // 512, 16))
    for p in range(k // 512):
        a[p, :8] = np.random.permutation(np.resize(levels, 8))
        for g in range(8):
            far = levels[np.abs(levels - a[p, g]) >= 10]
            a[p, g + 8] = far[np.random.randint(len(far))]
    return np.exp2(a.ravel()).repeat(32)


def f64(x):
    return np.asarray(x).astype(np.float64)


def striped(idx):
    return np.tile(idx.reshape(-1, 16).T, (8, 1)).astype(np.uint16)


def unstriped(offs):
    return offs[:16].T.reshape(-1).astype(np.int64)


E2M1 = np.array([0.0, 0.5, 1.0, 1.5, 2.0, 3.0, 4.0, 6.0, -0.0, -0.5, -1.0, -1.5, -2.0, -3.0, -4.0, -6.0])


def pack_weight(w, fmt):
    k, n = w.shape
    w = f64(np.asarray(w, np.float32).astype(ml_dtypes.bfloat16)).reshape(k // 32, 32, n)
    amax = np.abs(w).max(1)
    if fmt == "e4m3":
        byte = np.frexp(amax)[1] - 1 + 127 - 7
    else:
        mant, ex = np.frexp(amax / 6.0)
        byte = np.where(mant > 0.5, ex, ex - 1) + 127
    byte = np.clip(np.where(amax > 0, byte, 1), 1, 254)
    scaled = (w * np.exp2(127.0 - byte)[:, None, :]).reshape(k, n).astype(np.float32)
    by_word = np.ascontiguousarray(scaled.reshape(k // 512, 128, 4, n).transpose(0, 1, 3, 2))
    if fmt == "e4m3":
        words = by_word.astype(ml_dtypes.float8_e4m3fn).view(np.uint8)
    else:
        c = by_word.astype(ml_dtypes.float4_e2m1fn).view(np.uint8) & 0xF
        words = (c[..., 0::2] | (c[..., 1::2] << 4)).reshape(k // 512, 128, 2 * n)
    return np.ascontiguousarray(words), np.ascontiguousarray(byte.astype(np.uint8).reshape(k // 512, 16, n))


def unpack_weight(words, scales, fmt):
    g, _, n = scales.shape
    words = np.ascontiguousarray(words).reshape(g, 128, n, -1)
    if fmt == "e4m3":
        vals = words.view(ml_dtypes.float8_e4m3fn).astype(np.float64)
    else:
        nib = np.empty((g, 128, n, 4), np.uint8)
        nib[..., 0::2] = words & 0xF
        nib[..., 1::2] = words >> 4
        vals = E2M1[nib]
    vals = vals * np.repeat(np.exp2(scales.astype(np.float64) - 127.0), 8, axis=1)[..., None]
    return vals.transpose(0, 1, 3, 2).reshape(g * 512, n)


def gelu(v):
    return 0.5 * v * (1.0 + np.tanh(np.sqrt(2.0 / np.pi) * (v + 0.044715 * v**3)))


K, H, M, N, T, S, T2, P = 512, 1024, 512, 256, 4096, 1024, 2048, 512

def setup_inputs():
    n = np.random.standard_normal
    s, u, u2 = mx_kscale(K)[:, None], mx_kscale(H)[:, None], mx_kscale(M)[:, None]
    tab_words, tab_scales = pack_weight(n((K, T)) * s, "e4m3")
    w2_words, w2_scales = pack_weight(1.2 * n((H, M)) / np.sqrt(H) / u, "e2m1")
    perm = np.random.permutation(T2)
    return {
        "tab_words": tab_words, "tab_scales": tab_scales,
        "offs": striped(np.random.permutation(T)[:S]),
        "offs2": striped(np.random.permutation(T2)[:S]),
        "offs3": striped(perm[:P]),
        "offs4": striped(perm[P:2 * P]),
        "w1": (1.3 * n((K, H)) / np.sqrt(K) / s).astype(np.float32),
        "b1": (0.7 * n(H)).astype(np.float32),
        "gain": (1.2 * np.exp(0.3 * n(H)) * u[:, 0]).astype(np.float32),
        "wgs": np.exp(0.3 * n((128, S))).astype(np.float32),
        "page0": (n((H, T2)) * u).astype(np.float32),
        "w2_words": w2_words, "w2_scales": w2_scales,
        "gain2": (np.exp(0.3 * n(M)) * u2[:, 0]).astype(np.float32),
        "w3": (1.2 * n((M, N)) / np.sqrt(M) / u2).astype(np.float32),
        "b3": (0.7 * n(N)).astype(np.float32),
    }

def reference(tab_words, tab_scales, offs, offs2, offs3, offs4, w1, b1, gain, wgs, page0,
              w2_words, w2_scales, gain2, w3, b3):
    v = unpack_weight(tab_words, tab_scales, "e4m3")[:, unstriped(offs)]
    x = (mxq(f64(w1), 0, "e4m3").T @ v) + f64(b1)[:, None]
    h = f64(gain)[:, None] * (x / (1.0 + np.exp(-x)))
    page = f64(page0).copy()
    page[:, unstriped(offs2)] = np.tile(f64(wgs), (H // 128, 1)) * h
    a = page[:, unstriped(offs3)]
    b = page[:, unstriped(offs4)]
    page[:, unstriped(offs3)] = a + b
    page[:, unstriped(offs4)] = np.minimum(a, b)
    w2 = unpack_weight(w2_words, w2_scales, "e2m1")
    y = np.tanh(w2.T @ mxq(page, 0, "e4m3"))
    z = f64(gain2)[:, None] * y
    return (mxq(f64(w3), 0, "e4m3").T @ mxq(z, 0, "e4m3")) + f64(b3)[:, None]

@@ -1,0 +1,391 @@
+from contextlib import ExitStack
+
+import concourse.mybir as mybir
+
+K, H, M, N, T, S, T2, PAIRS = 512, 1024, 512, 256, 4096, 1024, 2048, 512
+FLOPS = 2 * (K * H * S + H * M * T2 + M * N * T2)
+
+F32 = mybir.dt.float32
+BF16 = mybir.dt.bfloat16
+I32 = mybir.dt.int32
+U32 = mybir.dt.uint32
+U16 = mybir.dt.uint16
+U8 = mybir.dt.uint8
+E4M3 = mybir.dt.float8_e4m3fn_x4
+E2M1 = mybir.dt.float4_e2m1fn_x4
+ALU = mybir.AluOpType
+ACT = mybir.ActivationFunctionType
+
+P = 128
+PACK = 4
+PASS = P * PACK
+HALF = S // 2
+TILES = H // P
+UNIT = 256
+UNITS = T2 // UNIT
+BANK_COLS = 128
+Y_BANKS = 6
+EARLY_UNITS = Y_BANKS * BANK_COLS // UNIT
+WIDE = 1024
+SCALAR_ROUND_UNITS = (1, 2)
+KIB = 1024
+
+
+def tile_list_corridor_preemption_page_kernel(
+    tc, tab_words, tab_scales, offs, offs2, offs3, offs4, w1, b1, gain, wgs, page0,
+    w2_words, w2_scales, gain2, w3, b3, out,
+):
+    nc = tc.nc
+    with ExitStack() as ctx:
+        keep = ctx.enter_context(tc.tile_pool(name="keep", bufs=1))
+        ring = ctx.enter_context(tc.tile_pool(name="ring", bufs=2))
+        shared = ctx.enter_context(tc.tile_pool(name="shared", bufs=1))
+        psum = ctx.enter_context(tc.psum_pool(name="psum", bufs=1))
+
+        def held(shape, dtype, name):
+            return keep.tile(shape, dtype, name=name, align_bytes=64)
+
+        def placed(shape, dtype, name, offset, bufs=1):
+            return shared.tile(shape, dtype, name=name, align_bytes=64, offset=offset, bufs=bufs)
+
+        list1 = keep.tile([P, S // 16], U16, name="list1")
+        list2 = keep.tile([P, S // 16], U16, name="list2")
+        list3 = keep.tile([P, PAIRS // 16], U16, name="list3")
+        list4 = keep.tile([P, PAIRS // 16], U16, name="list4")
+        tab_w = placed([P, T], U32, "tab_w", 0)
+        tab_s = placed([P, T], U8, "tab_s", 16 * KIB)
+        w1_raw = [placed([P, PACK, PASS], F32, f"w1_raw{b}", (20 + 8 * b) * KIB) for b in range(2)]
+        b1_sb = held([P, 2, PACK], F32, "b1_sb")
+        gain_sb = held([P, 2, PACK], F32, "gain_sb")
+        wgs_first = held([P, S], F32, "wgs_first")
+        wgs_second = held([P, S], F32, "wgs_second")
+        wgs_rest = held([P, 2, S], F32, "wgs_rest")
+        pages = [held([P, T2], F32, f"page{i}") for i in range(TILES)]
+        w2_w_raw = held([P, 2, 2 * M], U8, "w2_w_raw")
+        w2_s_raw = held([P, 2, M], U8, "w2_s_raw")
+        w3_raw = held([P, PACK, N], F32, "w3_raw")
+        gain2_sb = held([P, 1, PACK], F32, "gain2_sb")
+        b3_sb = held([P, 2], F32, "b3_sb")
+
+        page_rows = page0.rearrange("(b p t) c -> b t p c", b=2, t=PACK)
+        wgs_rows = wgs.rearrange("(p t) j -> p t j", t=PACK)
+        w1_rows = w1.rearrange("(p j) c -> p j c", j=PACK)
+
+        def load_page(i):
+            nc.sync.dma_start(out=pages[i][:], in_=page_rows[i // PACK, i % PACK])
+
+        def load_w1(b):
+            nc.sync.dma_start(out=w1_raw[b][:], in_=w1_rows[:, :, b * PASS : (b + 1) * PASS])
+
+        nc.vector.memset(tab_s[:].bitcast(I32), 0)
+        nc.vector.memset(w2_s_raw[:].rearrange("p a c -> p (a c)").bitcast(I32), 0)
+
+        nc.sync.dma_start(list1[:], offs)
+        load_w1(0)
+        for q in range(4):
+            nc.sync.dma_start(
+                out=tab_s[32 * q : 32 * q + 4, :].bitcast(I32),
+                in_=tab_scales[0, 4 * q : 4 * q + 4, :].bitcast(I32),
+            )
+        nc.sync.dma_start(
+            out=tab_w[:].bitcast(I32), in_=tab_words[0].rearrange("p c i -> p (c i)").bitcast(I32)
+        )
+        nc.sync.dma_start(out=b1_sb[:], in_=b1.rearrange("(b p t) -> p b t", b=2, t=PACK))
+        load_page(0)
+        nc.sync.dma_start(out=gain_sb[:], in_=gain.rearrange("(b p t) -> p b t", b=2, t=PACK))
+        nc.sync.dma_start(list2[:], offs2)
+        for q in range(4):
+            nc.sync.dma_start(out=wgs_first[32 * q : 32 * q + 32, :], in_=wgs_rows[:, 0, :])
+        nc.sync.dma_start(list3[:], offs3)
+        nc.sync.dma_start(list4[:], offs4)
+        load_page(1)
+        for q in range(4):
+            nc.sync.dma_start(out=wgs_second[32 * q : 32 * q + 32, :], in_=wgs_rows[:, 1, :])
+        load_w1(1)
+        load_page(2)
+        for q in range(4):
+            nc.sync.dma_start(out=wgs_rest[32 * q : 32 * q + 32, :, :], in_=wgs_rows[:, 2:PACK, :])
+        load_page(3)
+        w3_rows = w3.rearrange("(g t r) n -> r g t n", t=PACK, r=8)
+        for r in range(8):
+            nc.sync.dma_start(out=w3_raw[r:P:8, :, :], in_=w3_rows[r])
+        for i in range(PACK, TILES):
+            load_page(i)
+        nc.sync.dma_start(
+            out=w2_w_raw[:].bitcast(I32), in_=w2_words.rearrange("a p c -> p a c").bitcast(I32)
+        )
+        for q in range(4):
+            nc.sync.dma_start(
+                out=w2_s_raw[32 * q : 32 * q + 4, :, :].bitcast(I32),
+                in_=w2_scales[:, 4 * q : 4 * q + 4, :].rearrange("a r c -> r a c").bitcast(I32),
+            )
+        gain2_rows = gain2.rearrange("(g t r) -> r g t", t=PACK, r=8)
+        with nc.allow_non_contiguous_dma(reason="one value of a short vector to each partition"):
+            for r in range(8):
+                nc.sync.dma_start(out=gain2_sb[r:P:8, 0, :], in_=gain2_rows[r])
+            nc.sync.dma_start(out=b3_sb[:], in_=b3.rearrange("(h p) -> p h", p=P))
+
+        w1_bf = [placed([P, PACK, P, PACK], BF16, f"w1_bf{b}", (36 + 4 * b) * KIB) for b in range(2)]
+        w1_c = [held([P, PASS], U32, f"w1_c{b}") for b in range(2)]
+        w1_s = [held([P, PASS], U8, f"w1_s{b}") for b in range(2)]
+
+        def round_w1(b, t, on_vector):
+            source = w1_raw[b][:].rearrange("p j (m t) -> p t m j", t=PACK)[:, t]
+            if on_vector:
+                nc.vector.tensor_copy(out=w1_bf[b][:, t], in_=source)
+            else:
+                nc.scalar.copy(out=w1_bf[b][:, t], in_=source)
+
+        def quantize_w1(b):
+            nc.vector.quantize_mx(
+                out=w1_c[b][:].bitcast(E4M3), scales=w1_s[b][:],
+                in_=w1_bf[b][:].rearrange("p t m j -> p (t m j)"),
+            )
+
+        got_s = held([P, S], U8, "got_s")
+        got_w = [held([P, HALF], U32, f"got_w{u}") for u in range(2)]
+        for t in range(PACK):
+            round_w1(0, t, on_vector=t < 2)
+        nc.vector.tensor_copy(out=got_s[:], in_=tab_s[:].indirect(list1[:]))
+        quantize_w1(0)
+        for u in range(2):
+            nc.vector.tensor_copy(
+                out=got_w[u][:], in_=tab_w[:].indirect(list1[:, u * HALF // 16 : (u + 1) * HALF // 16])
+            )
+
+        states = {}
+
+        def make_states(i):
+            b, t = divmod(i, PACK)
+            if i in (0, TILES - 1):
+                halves = [keep.tile([P, HALF], F32, name="state", tag=f"state{i}_{u}", align_bytes=64)[:] for u in range(2)]
+            else:
+                states[i] = keep.tile([P, S], F32, name="state", tag=f"state{i}_0", align_bytes=64)
+                halves = [states[i][:, u * HALF : (u + 1) * HALF] for u in range(2)]
+            for u in range(2):
+                bank = psum.tile([P, HALF], F32, name="x_bank", tag=f"side{u}")
+                nc.tensor.matmul_mx(
+                    out=bank[:],
+                    lhsT=w1_c[b][:, t * P : (t + 1) * P].bitcast(E4M3),
+                    lhsT_scale=w1_s[b][:, t * P : (t + 1) * P],
+                    rhs=got_w[u][:].bitcast(E4M3),
+                    rhs_scale=got_s[:, u * HALF : (u + 1) * HALF],
+                    start=True, stop=True,
+                )
+                silu = ring.tile([P, HALF], F32, name="silu")
+                states[i, u] = halves[u]
+                nc.scalar.activation(out=silu[:], in_=bank[:], func=ACT.Silu, bias=b1_sb[:, b, t : t + 1])
+                nc.scalar.activation(
+                    out=states[i, u], in_=silu[:], func=ACT.Copy, scale=gain_sb[:, b, t : t + 1]
+                )
+
+        for i in range(PACK):
+            make_states(i)
+        for t in range(PACK):
+            round_w1(1, t, on_vector=False)
+
+        wgs_dealt = [wgs_first[:], wgs_second[:], wgs_rest[:, 0, :], wgs_rest[:, 1, :]]
+
+        def put_states(i):
+            nc.vector.tensor_tensor(pages[i][:].indirect(list2[:]), wgs_dealt[i % PACK], states[i][:], ALU.mult)
+
+        def put_half_states(i, u):
+            nc.vector.tensor_tensor(
+                pages[i][:].indirect(list2[:, u * HALF // 16 : (u + 1) * HALF // 16]),
+                wgs_dealt[i % PACK][:, u * HALF : (u + 1) * HALF], states[i, u], ALU.mult,
+            )
+
+        first_bf = [held([P, WIDE, PACK], BF16, f"first_bf{c}") for c in range(T2 // WIDE)]
+        first_c = {}
+        first_s = [held([P, WIDE], U8, f"first_s{c}") for c in range(T2 // WIDE)]
+        second_bf = [placed([P, UNIT, PACK], BF16, f"second_bf{c}", 2 * KIB * c) for c in range(UNITS)]
+        second_c = [placed([P, UNIT], U32, f"second_c{c}", (16 + c) * KIB) for c in range(UNITS)]
+        second_s = [placed([P, UNIT], U8, f"second_s{c}", 24 * KIB + UNIT * c) for c in range(UNITS)]
+
+        def round_page(i, c):
+            b, t = divmod(i, PACK)
+            width = UNIT if b else WIDE
+            target = second_bf[c] if b else first_bf[c]
+            source = pages[i][:, c * width : (c + 1) * width]
+            if i == TILES - 1 and c not in SCALAR_ROUND_UNITS:
+                nc.vector.tensor_copy(out=target[:, :, t], in_=source)
+            else:
+                nc.scalar.copy(out=target[:, :, t], in_=source)
+
+        def quantize_first(c):
+            tag = (f"state{TILES - 1}_1", f"state{TILES - 2}_0")[c]
+            first_c[c] = keep.tile([P, WIDE], U32, name="first_c", tag=tag, align_bytes=64)
+            nc.vector.quantize_mx(
+                out=first_c[c][:].bitcast(E4M3), scales=first_s[c][:],
+                in_=first_bf[c][:].rearrange("p c t -> p (c t)"),
+            )
+
+        def quantize_second(c):
+            nc.vector.quantize_mx(
+                out=second_c[c][:].bitcast(E4M3), scales=second_s[c][:],
+                in_=second_bf[c][:].rearrange("p c t -> p (c t)"),
+            )
+
+        w2_w = held([P, 2, 2 * M], U8, "w2_w")
+        w2_s = held([P, 2, M], U8, "w2_s")
+
+        def deal_w2():
+            for raw, dealt in ((w2_w_raw, w2_w), (w2_s_raw, w2_s)):
+                nc.vector.tensor_copy(
+                    out=dealt[:].bitcast(I32).rearrange("p a (t g e) -> p a t g e", t=PACK, g=16),
+                    in_=raw[:].bitcast(I32).rearrange("p a (g t e) -> p a t g e", t=PACK, g=16),
+                )
+
+        w3_bf = held([P, N, PACK], BF16, "w3_bf")
+        w3_codes = []
+        w3_s = held([P, N], U8, "w3_s")
+
+        def quantize_w3():
+            w3_c = keep.tile([P, N], U32, name="w3_c", tag=f"state{TILES - 1}_0", align_bytes=64)
+            w3_codes.append(w3_c)
+            nc.vector.quantize_mx(
+                out=w3_c[:].bitcast(E4M3), scales=w3_s[:], in_=w3_bf[:].rearrange("p n t -> p (n t)")
+            )
+
+        y_banks = {}
+
+        def second_stage_pass(block, b):
+            if b == 0:
+                y_banks[block] = psum.tile([P, PACK, BANK_COLS], F32, name="y_bank", tag=f"y{block % Y_BANKS}")
+            width = UNIT if b else WIDE
+            c, start = divmod(block * BANK_COLS, width)
+            codes, scales = (second_c[c], second_s[c]) if b else (first_c[c], first_s[c])
+            for t in range(PACK):
+                nc.tensor.matmul_mx(
+                    out=y_banks[block][:, t, :],
+                    lhsT=w2_w[:, b, 2 * t * P : 2 * (t + 1) * P].bitcast(E2M1),
+                    lhsT_scale=w2_s[:, b, t * P : (t + 1) * P],
+                    rhs=codes[:, start : start + BANK_COLS].bitcast(E4M3),
+                    rhs_scale=scales[:, start : start + BANK_COLS],
+                    start=(b == 0 and t == 0), stop=(b == 1 and t == PACK - 1),
+                )
+
+        quantize_w1(1)
+        for i in range(PACK, TILES):
+            make_states(i)
+        nc.scalar.copy(out=w3_bf[:], in_=w3_raw[:].rearrange("p t n -> p n t"))
+
+        one, other, least = {}, {}, {}
+
+        def fetch_one(i):
+            if i % 2 == 0 and i < TILES - 2:
+                one[i] = keep.tile([P, PAIRS], F32, name="one", tag=f"state{i + 1}_0", align_bytes=64)
+            else:
+                one[i] = ring.tile([P, PAIRS], F32, name="one_odd", bufs=1)
+            nc.vector.tensor_copy(out=one[i][:], in_=pages[i][:].indirect(list3[:]))
+
+        def fetch_other(i):
+            other[i] = ring.tile([P, PAIRS], F32, name="other")
+            nc.vector.tensor_copy(out=other[i][:], in_=pages[i][:].indirect(list4[:]))
+
+        def take_least(i):
+            if i == TILES - 1:
+                least[i] = keep.tile([P, PAIRS], F32, name="least_last", tag=f"page{i - 1}", align_bytes=64)
+            else:
+                least[i] = ring.tile([P, PAIRS], F32, name="least")
+            nc.vector.tensor_tensor(least[i][:], one[i][:], other[i][:], ALU.min)
+
+        def put_sum(i):
+            nc.vector.tensor_tensor(pages[i][:].indirect(list3[:]), one[i][:], other[i][:], ALU.add)
+
+        def put_least(i):
+            nc.vector.tensor_copy(out=pages[i][:].indirect(list4[:]), in_=least[i][:])
+            if i < TILES - 1:
+                for c in range(T2 // WIDE if i < PACK else UNITS):
+                    round_page(i, c)
+
+        put_half_states(0, 0)
+        put_half_states(0, 1)
+        put_states(1)
+        for a in range(0, TILES - 2, 2):
+            for work in (fetch_one, fetch_other):
+                work(a)
+            for work in (fetch_one, fetch_other):
+                work(a + 1)
+            for work in (take_least, put_sum):
+                work(a)
+                work(a + 1)
+            put_least(a)
+            put_states(a + 2)
+            if a + 3 < TILES - 1:
+                put_states(a + 3)
+            put_least(a + 1)
+        a, b = TILES - 2, TILES - 1
+        fetch_one(a)
+        fetch_other(a)
+        put_half_states(b, 0)
+        take_least(a)
+        put_sum(a)
+        put_half_states(b, 1)
+        put_least(a)
+        fetch_one(b)
+        fetch_other(b)
+        deal_w2()
+        quantize_first(0)
+        for block in range(Y_BANKS):
+            second_stage_pass(block, 0)
+        put_sum(b)
+        take_least(b)
+        quantize_w3()
+        quantize_first(1)
+        put_least(b)
+
+        blocks_per_unit = UNIT // BANK_COLS
+        tanh_sb, z_bf, z_c, z_s = {}, {}, {}, {}
+        out_rows = out.rearrange("(h p) c -> p h c", p=P)
+
+        def second_stage(c):
+            tanh_sb[c] = placed([P, UNIT, PACK], F32, "tanh_sb", 26 * KIB, bufs=3)
+            for k in range(blocks_per_unit):
+                block = c * blocks_per_unit + k
+                if c >= EARLY_UNITS:
+                    second_stage_pass(block, 0)
+                second_stage_pass(block, 1)
+                nc.scalar.activation(
+                    out=tanh_sb[c][:, k * BANK_COLS : (k + 1) * BANK_COLS, :],
+                    in_=y_banks[block][:].rearrange("p t c -> p c t"), func=ACT.Tanh,
+                )
+
+        def apply_gain2(c):
+            z_bf[c] = ring.tile([P, UNIT, PACK], BF16, name="z_bf", align_bytes=64)
+            nc.vector.tensor_tensor(
+                z_bf[c][:], tanh_sb[c][:], gain2_sb[:].to_broadcast([P, UNIT, PACK]), ALU.mult
+            )
+
+        def quantize_z(c):
+            z_c[c] = ring.tile([P, UNIT], U32, name="z_c", align_bytes=64)
+            z_s[c] = ring.tile([P, UNIT], U8, name="z_s", align_bytes=64)
+            nc.vector.quantize_mx(
+                out=z_c[c][:].bitcast(E4M3), scales=z_s[c][:], in_=z_bf[c][:].rearrange("p c t -> p (c t)")
+            )
+
+        def third_stage(c):
+            bank = psum.tile([P, 2, UNIT], F32, name="o_bank", tag=f"side{c % 2}")
+            for h in range(2):
+                nc.tensor.matmul_mx(
+                    out=bank[:, h, :],
+                    lhsT=w3_codes[0][:, h * P : (h + 1) * P].bitcast(E4M3),
+                    lhsT_scale=w3_s[:, h * P : (h + 1) * P],
+                    rhs=z_c[c][:].bitcast(E4M3), rhs_scale=z_s[c][:],
+                    start=True, stop=True,
+                )
+            result = placed([P, 2, UNIT], F32, "result", 38 * KIB, bufs=3)
+            for h in range(2):
+                nc.scalar.activation(
+                    out=result[:, h, :], in_=bank[:, h, :], func=ACT.Identity, bias=b3_sb[:, h : h + 1]
+                )
+            nc.sync.dma_start(out=out_rows[:, :, c * UNIT : (c + 1) * UNIT], in_=result[:])
+
+        steps = (
+            (0, lambda c: round_page(TILES - 1, c)), (3, quantize_second), (3, second_stage), (5, apply_gain2),
+            (6, quantize_z), (6, third_stage),
+        )
+        for step in range(UNITS + 6):
+            for lag, work in steps:
+                if 0 <= step - lag < UNITS:
+                    work(step - lag)

@@ -29,6 +29,7 @@ EARLY_UNITS = Y_BANKS * BANK_COLS // UNIT
 WIDE = 1024
 SCALAR_ROUND_UNITS = (1, 2)
 KIB = 1024
+PIECES = {0: ((0, HALF // 2), (HALF // 2, HALF), (HALF, S)), TILES - 1: ((0, HALF), (HALF, S))}
 
 
 def tile_list_corridor_preemption_page_kernel(
@@ -81,6 +82,8 @@ def tile_list_corridor_preemption_page_kernel(
         nc.vector.memset(w2_s_raw[:].rearrange("p a c -> p (a c)").bitcast(I32), 0)
 
         nc.sync.dma_start(list1[:], offs)
+        nc.scalar.dma_start(out=b1_sb[:], in_=b1.rearrange("(b p t) -> p b t", b=2, t=PACK))
+        nc.scalar.dma_start(out=gain_sb[:], in_=gain.rearrange("(b p t) -> p b t", b=2, t=PACK))
         load_w1(0)
         for q in range(4):
             nc.sync.dma_start(
@@ -90,12 +93,14 @@ def tile_list_corridor_preemption_page_kernel(
         nc.sync.dma_start(
             out=tab_w[:].bitcast(I32), in_=tab_words[0].rearrange("p c i -> p (c i)").bitcast(I32)
         )
-        nc.sync.dma_start(out=b1_sb[:], in_=b1.rearrange("(b p t) -> p b t", b=2, t=PACK))
-        load_page(0)
-        nc.sync.dma_start(out=gain_sb[:], in_=gain.rearrange("(b p t) -> p b t", b=2, t=PACK))
         nc.sync.dma_start(list2[:], offs2)
-        for q in range(4):
-            nc.sync.dma_start(out=wgs_first[32 * q : 32 * q + 32, :], in_=wgs_rows[:, 0, :])
+        load_page(0)
+        for u in range(2):
+            for q in range(4):
+                nc.sync.dma_start(
+                    out=wgs_first[32 * q : 32 * q + 32, u * HALF : (u + 1) * HALF],
+                    in_=wgs_rows[:, 0, u * HALF : (u + 1) * HALF],
+                )
         nc.sync.dma_start(list3[:], offs3)
         nc.sync.dma_start(list4[:], offs4)
         load_page(1)
@@ -155,29 +160,33 @@ def tile_list_corridor_preemption_page_kernel(
 
         states = {}
 
-        def make_states(i):
+        def make_state_columns(i, lo, hi, target, bank_tag):
             b, t = divmod(i, PACK)
-            if i in (0, TILES - 1):
-                halves = [keep.tile([P, HALF], F32, name="state", tag=f"state{i}_{u}", align_bytes=64)[:] for u in range(2)]
+            u = lo // HALF
+            bank = psum.tile([P, hi - lo], F32, name="x_bank", tag=bank_tag)
+            nc.tensor.matmul_mx(
+                out=bank[:],
+                lhsT=w1_c[b][:, t * P : (t + 1) * P].bitcast(E4M3),
+                lhsT_scale=w1_s[b][:, t * P : (t + 1) * P],
+                rhs=got_w[u][:, lo - u * HALF : hi - u * HALF].bitcast(E4M3),
+                rhs_scale=got_s[:, lo:hi],
+                start=True, stop=True,
+            )
+            silu = ring.tile([P, hi - lo], F32, name="silu")
+            nc.scalar.activation(out=silu[:], in_=bank[:], func=ACT.Silu, bias=b1_sb[:, b, t : t + 1])
+            nc.scalar.activation(out=target, in_=silu[:], func=ACT.Copy, scale=gain_sb[:, b, t : t + 1])
+
+        def make_states(i):
+            if i in PIECES:
+                for k, (lo, hi) in enumerate(PIECES[i]):
+                    states[i, k] = keep.tile([P, hi - lo], F32, name="state", tag=f"state{i}_{k}", align_bytes=64)
+                    make_state_columns(i, lo, hi, states[i, k][:], ("side0", "side1", "y0")[k])
             else:
                 states[i] = keep.tile([P, S], F32, name="state", tag=f"state{i}_0", align_bytes=64)
-                halves = [states[i][:, u * HALF : (u + 1) * HALF] for u in range(2)]
-            for u in range(2):
-                bank = psum.tile([P, HALF], F32, name="x_bank", tag=f"side{u}")
-                nc.tensor.matmul_mx(
-                    out=bank[:],
-                    lhsT=w1_c[b][:, t * P : (t + 1) * P].bitcast(E4M3),
-                    lhsT_scale=w1_s[b][:, t * P : (t + 1) * P],
-                    rhs=got_w[u][:].bitcast(E4M3),
-                    rhs_scale=got_s[:, u * HALF : (u + 1) * HALF],
-                    start=True, stop=True,
-                )
-                silu = ring.tile([P, HALF], F32, name="silu")
-                states[i, u] = halves[u]
-                nc.scalar.activation(out=silu[:], in_=bank[:], func=ACT.Silu, bias=b1_sb[:, b, t : t + 1])
-                nc.scalar.activation(
-                    out=states[i, u], in_=silu[:], func=ACT.Copy, scale=gain_sb[:, b, t : t + 1]
-                )
+                for u in range(2):
+                    make_state_columns(
+                        i, u * HALF, (u + 1) * HALF, states[i][:, u * HALF : (u + 1) * HALF], f"side{u}"
+                    )
 
         for i in range(PACK):
             make_states(i)
@@ -186,14 +195,16 @@ def tile_list_corridor_preemption_page_kernel(
 
         wgs_dealt = [wgs_first[:], wgs_second[:], wgs_rest[:, 0, :], wgs_rest[:, 1, :]]
 
-        def put_states(i):
-            nc.vector.tensor_tensor(pages[i][:].indirect(list2[:]), wgs_dealt[i % PACK], states[i][:], ALU.mult)
-
-        def put_half_states(i, u):
+        def put_columns(i, lo, hi, values):
             nc.vector.tensor_tensor(
-                pages[i][:].indirect(list2[:, u * HALF // 16 : (u + 1) * HALF // 16]),
-                wgs_dealt[i % PACK][:, u * HALF : (u + 1) * HALF], states[i, u], ALU.mult,
+                pages[i][:].indirect(list2[:, lo // 16 : hi // 16]), wgs_dealt[i % PACK][:, lo:hi], values, ALU.mult
             )
+
+        def put_states(i):
+            put_columns(i, 0, S, states[i][:])
+
+        def put_piece(i, k):
+            put_columns(i, *PIECES[i][k], states[i, k][:])
 
         first_bf = [held([P, WIDE, PACK], BF16, f"first_bf{c}") for c in range(T2 // WIDE)]
         first_c = {}
@@ -213,7 +224,7 @@ def tile_list_corridor_preemption_page_kernel(
                 nc.scalar.copy(out=target[:, :, t], in_=source)
 
         def quantize_first(c):
-            tag = (f"state{TILES - 1}_1", f"state{TILES - 2}_0")[c]
+            tag = ("least_late", f"state{TILES - 1}_1")[c]
             first_c[c] = keep.tile([P, WIDE], U32, name="first_c", tag=tag, align_bytes=64)
             nc.vector.quantize_mx(
                 out=first_c[c][:].bitcast(E4M3), scales=first_s[c][:],
@@ -286,6 +297,8 @@ def tile_list_corridor_preemption_page_kernel(
         def take_least(i):
             if i == TILES - 1:
                 least[i] = keep.tile([P, PAIRS], F32, name="least_last", tag=f"page{i - 1}", align_bytes=64)
+            elif i == TILES - 2:
+                least[i] = keep.tile([P, PAIRS], F32, name="least_late", tag="least_late", align_bytes=64)
             else:
                 least[i] = ring.tile([P, PAIRS], F32, name="least")
             nc.vector.tensor_tensor(least[i][:], one[i][:], other[i][:], ALU.min)
@@ -299,8 +312,8 @@ def tile_list_corridor_preemption_page_kernel(
                 for c in range(T2 // WIDE if i < PACK else UNITS):
                     round_page(i, c)
 
-        put_half_states(0, 0)
-        put_half_states(0, 1)
+        for k in range(len(PIECES[0])):
+            put_piece(0, k)
         put_states(1)
         for a in range(0, TILES - 2, 2):
             for work in (fetch_one, fetch_other):
@@ -318,29 +331,35 @@ def tile_list_corridor_preemption_page_kernel(
         a, b = TILES - 2, TILES - 1
         fetch_one(a)
         fetch_other(a)
-        put_half_states(b, 0)
+        put_piece(b, 0)
         take_least(a)
         put_sum(a)
-        put_half_states(b, 1)
+        put_piece(b, 1)
         put_least(a)
         fetch_one(b)
         fetch_other(b)
         deal_w2()
+        quantize_w3()
+        quantize_first(1)
+        put_sum(b)
+        take_least(b)
         quantize_first(0)
         for block in range(Y_BANKS):
             second_stage_pass(block, 0)
-        put_sum(b)
-        take_least(b)
-        quantize_w3()
-        quantize_first(1)
         put_least(b)
 
         blocks_per_unit = UNIT // BANK_COLS
-        tanh_sb, z_bf, z_c, z_s = {}, {}, {}, {}
+        tanh_sb, z_bf, banks = {}, {}, {}
         out_rows = out.rearrange("(h p) c -> p h c", p=P)
+        spans = [(c * UNIT, UNIT) for c in range(UNITS - 1)]
+        spans = spans + [(T2 - UNIT, BANK_COLS), (T2 - BANK_COLS, BANK_COLS)]
+        out_tags = ["side0", "side1", "y4", "y5", "y0", "y1", "y2", "y3"]
 
         def second_stage(c):
-            tanh_sb[c] = placed([P, UNIT, PACK], F32, "tanh_sb", 26 * KIB, bufs=3)
+            if c < TILES - 2:
+                tanh_sb[c] = keep.tile([P, UNIT, PACK], F32, name="tanh_sb", tag=f"page{c}", align_bytes=64)
+            else:
+                tanh_sb[c] = placed([P, UNIT, PACK], F32, f"tanh_late{c}", (26 + 4 * (c - TILES + 2)) * KIB)
             for k in range(blocks_per_unit):
                 block = c * blocks_per_unit + k
                 if c >= EARLY_UNITS:
@@ -351,41 +370,61 @@ def tile_list_corridor_preemption_page_kernel(
                     in_=y_banks[block][:].rearrange("p t c -> p c t"), func=ACT.Tanh,
                 )
 
-        def apply_gain2(c):
-            z_bf[c] = ring.tile([P, UNIT, PACK], BF16, name="z_bf", align_bytes=64)
+        def apply_gain2(k):
+            start, width = spans[k]
+            c, inner = divmod(start, UNIT)
+            z_bf[k] = ring.tile([P, width, PACK], BF16, name="z_bf", align_bytes=64, bufs=3)
             nc.vector.tensor_tensor(
-                z_bf[c][:], tanh_sb[c][:], gain2_sb[:].to_broadcast([P, UNIT, PACK]), ALU.mult
+                z_bf[k][:], tanh_sb[c][:, inner : inner + width, :],
+                gain2_sb[:].to_broadcast([P, width, PACK]), ALU.mult,
             )
 
-        def quantize_z(c):
-            z_c[c] = ring.tile([P, UNIT], U32, name="z_c", align_bytes=64)
-            z_s[c] = ring.tile([P, UNIT], U8, name="z_s", align_bytes=64)
+        def third_stage(k):
+            width = spans[k][1]
+            z_c = ring.tile([P, width], U32, name="z_c", align_bytes=64)
+            z_s = ring.tile([P, width], U8, name="z_s", align_bytes=64)
             nc.vector.quantize_mx(
-                out=z_c[c][:].bitcast(E4M3), scales=z_s[c][:], in_=z_bf[c][:].rearrange("p c t -> p (c t)")
+                out=z_c[:].bitcast(E4M3), scales=z_s[:], in_=z_bf[k][:].rearrange("p c t -> p (c t)")
             )
-
-        def third_stage(c):
-            bank = psum.tile([P, 2, UNIT], F32, name="o_bank", tag=f"side{c % 2}")
+            if k < len(out_tags):
+                both = psum.tile([P, 2, width], F32, name="o_bank", tag=out_tags[k])
+                banks[k] = [both[:, h, :] for h in range(2)]
+            else:
+                banks[k] = [psum.tile([P, width], F32, name="o_half", tag=f"side{h}")[:] for h in range(2)]
             for h in range(2):
                 nc.tensor.matmul_mx(
-                    out=bank[:, h, :],
+                    out=banks[k][h],
                     lhsT=w3_codes[0][:, h * P : (h + 1) * P].bitcast(E4M3),
                     lhsT_scale=w3_s[:, h * P : (h + 1) * P],
-                    rhs=z_c[c][:].bitcast(E4M3), rhs_scale=z_s[c][:],
+                    rhs=z_c[:].bitcast(E4M3), rhs_scale=z_s[:],
                     start=True, stop=True,
                 )
-            result = placed([P, 2, UNIT], F32, "result", 38 * KIB, bufs=3)
-            for h in range(2):
-                nc.scalar.activation(
-                    out=result[:, h, :], in_=bank[:, h, :], func=ACT.Identity, bias=b3_sb[:, h : h + 1]
-                )
-            nc.sync.dma_start(out=out_rows[:, :, c * UNIT : (c + 1) * UNIT], in_=result[:])
 
-        steps = (
-            (0, lambda c: round_page(TILES - 1, c)), (3, quantize_second), (3, second_stage), (5, apply_gain2),
-            (6, quantize_z), (6, third_stage),
-        )
-        for step in range(UNITS + 6):
-            for lag, work in steps:
-                if 0 <= step - lag < UNITS:
-                    work(step - lag)
+        def store(k):
+            start, width = spans[k]
+            result = placed([P, 2, width], F32, f"result{k}", (34 + 2 * k) * KIB)
+            for h in range(2):
+                if k == len(spans) - 1 and h == 1:
+                    nc.vector.tensor_scalar(result[:, h, :], banks[k][h], b3_sb[:, h : h + 1], None, ALU.add)
+                else:
+                    nc.scalar.activation(
+                        out=result[:, h, :], in_=banks[k][h], func=ACT.Identity, bias=b3_sb[:, h : h + 1]
+                    )
+            nc.sync.dma_start(out=out_rows[:, :, start : start + width], in_=result[:])
+
+        round_lead = 4
+        for step in range(UNITS + round_lead):
+            if step < UNITS:
+                round_page(TILES - 1, step)
+            if step >= round_lead - 1 and step - round_lead + 1 < UNITS:
+                quantize_second(step - round_lead + 1)
+                second_stage(step - round_lead + 1)
+        apply_gain2(0)
+        for k in range(len(spans) - 1):
+            apply_gain2(k + 1)
+            third_stage(k)
+        store(0)
+        store(1)
+        third_stage(len(spans) - 1)
+        for k in range(2, len(spans)):
+            store(k)

@@ -85,18 +85,15 @@ def tile_list_corridor_preemption_page_kernel(
         nc.scalar.dma_start(out=b1_sb[:], in_=b1.rearrange("(b p t) -> p b t", b=2, t=PACK))
         nc.scalar.dma_start(out=gain_sb[:], in_=gain.rearrange("(b p t) -> p b t", b=2, t=PACK))
         load_w1(0)
-        for q in range(4):
-            nc.sync.dma_start(
-                out=tab_s[32 * q : 32 * q + 4, :].bitcast(I32),
-                in_=tab_scales[0, 4 * q : 4 * q + 4, :].bitcast(I32),
-            )
+        for r in range(4):
+            nc.sync.dma_start(out=tab_s[r:P:32, :].bitcast(I32), in_=tab_scales[0, r:16:4, :].bitcast(I32))
         nc.sync.dma_start(
             out=tab_w[:].bitcast(I32), in_=tab_words[0].rearrange("p c i -> p (c i)").bitcast(I32)
         )
         nc.sync.dma_start(list2[:], offs2)
         load_page(0)
         for u in range(2):
-            for q in range(4):
+            for q in (0, 2, 1, 3):
                 nc.sync.dma_start(
                     out=wgs_first[32 * q : 32 * q + 32, u * HALF : (u + 1) * HALF],
                     in_=wgs_rows[:, 0, u * HALF : (u + 1) * HALF],
@@ -353,7 +350,7 @@ def tile_list_corridor_preemption_page_kernel(
         out_rows = out.rearrange("(h p) c -> p h c", p=P)
         spans = [(c * UNIT, UNIT) for c in range(UNITS - 1)]
         spans = spans + [(T2 - UNIT, BANK_COLS), (T2 - BANK_COLS, BANK_COLS)]
-        out_tags = ["side0", "side1", "y4", "y5", "y0", "y1", "y2", "y3"]
+        out_tags = ["side0", "side1"] * 3 + ["y4", "y5"]
 
         def second_stage(c):
             if c < TILES - 2:
@@ -390,7 +387,7 @@ def tile_list_corridor_preemption_page_kernel(
                 both = psum.tile([P, 2, width], F32, name="o_bank", tag=out_tags[k])
                 banks[k] = [both[:, h, :] for h in range(2)]
             else:
-                banks[k] = [psum.tile([P, width], F32, name="o_half", tag=f"side{h}")[:] for h in range(2)]
+                banks[k] = [psum.tile([P, width], F32, name="o_half", tag=f"y{h}")[:] for h in range(2)]
             for h in range(2):
                 nc.tensor.matmul_mx(
                     out=banks[k][h],
@@ -412,19 +409,19 @@ def tile_list_corridor_preemption_page_kernel(
                     )
             nc.sync.dma_start(out=out_rows[:, :, start : start + width], in_=result[:])
 
-        round_lead = 4
+        round_lead, tanh_lead = 3, 4
         for step in range(UNITS + round_lead):
             if step < UNITS:
                 round_page(TILES - 1, step)
-            if step >= round_lead - 1 and step - round_lead + 1 < UNITS:
-                quantize_second(step - round_lead + 1)
-                second_stage(step - round_lead + 1)
+            if step >= round_lead:
+                quantize_second(step - round_lead)
+                if step - round_lead < tanh_lead:
+                    second_stage(step - round_lead)
         apply_gain2(0)
-        for k in range(len(spans) - 1):
-            apply_gain2(k + 1)
+        for k in range(len(spans)):
+            if k + 1 < len(spans):
+                apply_gain2(k + 1)
             third_stage(k)
-        store(0)
-        store(1)
-        third_stage(len(spans) - 1)
-        for k in range(2, len(spans)):
             store(k)
+            if k + tanh_lead < UNITS:
+                second_stage(k + tanh_lead)

from contextlib import ExitStack

import concourse.mybir as mybir

K, H, M, N, T, S, T2, PAIRS = 512, 1024, 512, 256, 4096, 1024, 2048, 512
FLOPS = 2 * (K * H * S + H * M * T2 + M * N * T2)

F32 = mybir.dt.float32
BF16 = mybir.dt.bfloat16
I32 = mybir.dt.int32
U32 = mybir.dt.uint32
U16 = mybir.dt.uint16
U8 = mybir.dt.uint8
E4M3 = mybir.dt.float8_e4m3fn_x4
E2M1 = mybir.dt.float4_e2m1fn_x4
ALU = mybir.AluOpType
ACT = mybir.ActivationFunctionType

P = 128
PACK = 4
PASS = P * PACK
HALF = S // 2
TILES = H // P
UNIT = 256
UNITS = T2 // UNIT
BANK_COLS = 128
Y_BANKS = 6
EARLY_UNITS = Y_BANKS * BANK_COLS // UNIT
WIDE = 1024
SCALAR_ROUND_UNITS = (1, 2)
KIB = 1024
PIECES = {0: ((0, HALF // 2), (HALF // 2, HALF), (HALF, S)), TILES - 1: ((0, HALF), (HALF, S))}


def tile_list_corridor_preemption_page_kernel(
    tc, tab_words, tab_scales, offs, offs2, offs3, offs4, w1, b1, gain, wgs, page0,
    w2_words, w2_scales, gain2, w3, b3, out,
):
    nc = tc.nc
    with ExitStack() as ctx:
        keep = ctx.enter_context(tc.tile_pool(name="keep", bufs=1))
        ring = ctx.enter_context(tc.tile_pool(name="ring", bufs=2))
        shared = ctx.enter_context(tc.tile_pool(name="shared", bufs=1))
        psum = ctx.enter_context(tc.psum_pool(name="psum", bufs=1))

        def held(shape, dtype, name):
            return keep.tile(shape, dtype, name=name, align_bytes=64)

        def placed(shape, dtype, name, offset, bufs=1):
            return shared.tile(shape, dtype, name=name, align_bytes=64, offset=offset, bufs=bufs)

        list1 = keep.tile([P, S // 16], U16, name="list1")
        list2 = keep.tile([P, S // 16], U16, name="list2")
        list3 = keep.tile([P, PAIRS // 16], U16, name="list3")
        list4 = keep.tile([P, PAIRS // 16], U16, name="list4")
        tab_w = placed([P, T], U32, "tab_w", 0)
        tab_s = placed([P, T], U8, "tab_s", 16 * KIB)
        w1_raw = [placed([P, PACK, PASS], F32, f"w1_raw{b}", (20 + 8 * b) * KIB) for b in range(2)]
        b1_sb = held([P, 2, PACK], F32, "b1_sb")
        gain_sb = held([P, 2, PACK], F32, "gain_sb")
        wgs_first = held([P, S], F32, "wgs_first")
        wgs_second = held([P, S], F32, "wgs_second")
        wgs_rest = held([P, 2, S], F32, "wgs_rest")
        pages = [held([P, T2], F32, f"page{i}") for i in range(TILES)]
        w2_w_raw = held([P, 2, 2 * M], U8, "w2_w_raw")
        w2_s_raw = held([P, 2, M], U8, "w2_s_raw")
        w3_raw = held([P, PACK, N], F32, "w3_raw")
        gain2_sb = held([P, 1, PACK], F32, "gain2_sb")
        b3_sb = held([P, 2], F32, "b3_sb")

        page_rows = page0.rearrange("(b p t) c -> b t p c", b=2, t=PACK)
        wgs_rows = wgs.rearrange("(p t) j -> p t j", t=PACK)
        w1_rows = w1.rearrange("(p j) c -> p j c", j=PACK)

        def load_page(i):
            nc.sync.dma_start(out=pages[i][:], in_=page_rows[i // PACK, i % PACK])

        def load_w1(b):
            nc.sync.dma_start(out=w1_raw[b][:], in_=w1_rows[:, :, b * PASS : (b + 1) * PASS])

        nc.vector.memset(tab_s[:].bitcast(I32), 0)
        nc.vector.memset(w2_s_raw[:].rearrange("p a c -> p (a c)").bitcast(I32), 0)

        nc.sync.dma_start(list1[:], offs)
        nc.scalar.dma_start(out=b1_sb[:], in_=b1.rearrange("(b p t) -> p b t", b=2, t=PACK))
        nc.scalar.dma_start(out=gain_sb[:], in_=gain.rearrange("(b p t) -> p b t", b=2, t=PACK))
        load_w1(0)
        for r in range(4):
            nc.sync.dma_start(out=tab_s[r:P:32, :].bitcast(I32), in_=tab_scales[0, r:16:4, :].bitcast(I32))
        nc.sync.dma_start(
            out=tab_w[:].bitcast(I32), in_=tab_words[0].rearrange("p c i -> p (c i)").bitcast(I32)
        )
        nc.sync.dma_start(list2[:], offs2)
        load_page(0)
        for u in range(2):
            for q in (0, 2, 1, 3):
                nc.sync.dma_start(
                    out=wgs_first[32 * q : 32 * q + 32, u * HALF : (u + 1) * HALF],
                    in_=wgs_rows[:, 0, u * HALF : (u + 1) * HALF],
                )
        nc.sync.dma_start(list3[:], offs3)
        nc.sync.dma_start(list4[:], offs4)
        load_page(1)
        for q in range(4):
            nc.sync.dma_start(out=wgs_second[32 * q : 32 * q + 32, :], in_=wgs_rows[:, 1, :])
        load_w1(1)
        load_page(2)
        for q in range(4):
            nc.sync.dma_start(out=wgs_rest[32 * q : 32 * q + 32, :, :], in_=wgs_rows[:, 2:PACK, :])
        load_page(3)
        w3_rows = w3.rearrange("(g t r) n -> r g t n", t=PACK, r=8)
        for r in range(8):
            nc.sync.dma_start(out=w3_raw[r:P:8, :, :], in_=w3_rows[r])
        for i in range(PACK, TILES):
            load_page(i)
        nc.sync.dma_start(
            out=w2_w_raw[:].bitcast(I32), in_=w2_words.rearrange("a p c -> p a c").bitcast(I32)
        )
        for q in range(4):
            nc.sync.dma_start(
                out=w2_s_raw[32 * q : 32 * q + 4, :, :].bitcast(I32),
                in_=w2_scales[:, 4 * q : 4 * q + 4, :].rearrange("a r c -> r a c").bitcast(I32),
            )
        gain2_rows = gain2.rearrange("(g t r) -> r g t", t=PACK, r=8)
        with nc.allow_non_contiguous_dma(reason="one value of a short vector to each partition"):
            for r in range(8):
                nc.sync.dma_start(out=gain2_sb[r:P:8, 0, :], in_=gain2_rows[r])
            nc.sync.dma_start(out=b3_sb[:], in_=b3.rearrange("(h p) -> p h", p=P))

        w1_bf = [placed([P, PACK, P, PACK], BF16, f"w1_bf{b}", (36 + 4 * b) * KIB) for b in range(2)]
        w1_c = [held([P, PASS], U32, f"w1_c{b}") for b in range(2)]
        w1_s = [held([P, PASS], U8, f"w1_s{b}") for b in range(2)]

        def round_w1(b, t, on_vector):
            source = w1_raw[b][:].rearrange("p j (m t) -> p t m j", t=PACK)[:, t]
            if on_vector:
                nc.vector.tensor_copy(out=w1_bf[b][:, t], in_=source)
            else:
                nc.scalar.copy(out=w1_bf[b][:, t], in_=source)

        def quantize_w1(b):
            nc.vector.quantize_mx(
                out=w1_c[b][:].bitcast(E4M3), scales=w1_s[b][:],
                in_=w1_bf[b][:].rearrange("p t m j -> p (t m j)"),
            )

        got_s = held([P, S], U8, "got_s")
        got_w = [held([P, HALF], U32, f"got_w{u}") for u in range(2)]
        for t in range(PACK):
            round_w1(0, t, on_vector=t < 2)
        nc.vector.tensor_copy(out=got_s[:], in_=tab_s[:].indirect(list1[:]))
        quantize_w1(0)
        for u in range(2):
            nc.vector.tensor_copy(
                out=got_w[u][:], in_=tab_w[:].indirect(list1[:, u * HALF // 16 : (u + 1) * HALF // 16])
            )

        states = {}

        def make_state_columns(i, lo, hi, target, bank_tag):
            b, t = divmod(i, PACK)
            u = lo // HALF
            bank = psum.tile([P, hi - lo], F32, name="x_bank", tag=bank_tag)
            nc.tensor.matmul_mx(
                out=bank[:],
                lhsT=w1_c[b][:, t * P : (t + 1) * P].bitcast(E4M3),
                lhsT_scale=w1_s[b][:, t * P : (t + 1) * P],
                rhs=got_w[u][:, lo - u * HALF : hi - u * HALF].bitcast(E4M3),
                rhs_scale=got_s[:, lo:hi],
                start=True, stop=True,
            )
            silu = ring.tile([P, hi - lo], F32, name="silu")
            nc.scalar.activation(out=silu[:], in_=bank[:], func=ACT.Silu, bias=b1_sb[:, b, t : t + 1])
            nc.scalar.activation(out=target, in_=silu[:], func=ACT.Copy, scale=gain_sb[:, b, t : t + 1])

        def make_states(i):
            if i in PIECES:
                for k, (lo, hi) in enumerate(PIECES[i]):
                    states[i, k] = keep.tile([P, hi - lo], F32, name="state", tag=f"state{i}_{k}", align_bytes=64)
                    make_state_columns(i, lo, hi, states[i, k][:], ("side0", "side1", "y0")[k])
            else:
                states[i] = keep.tile([P, S], F32, name="state", tag=f"state{i}_0", align_bytes=64)
                for u in range(2):
                    make_state_columns(
                        i, u * HALF, (u + 1) * HALF, states[i][:, u * HALF : (u + 1) * HALF], f"side{u}"
                    )

        for i in range(PACK):
            make_states(i)
        for t in range(PACK):
            round_w1(1, t, on_vector=False)

        wgs_dealt = [wgs_first[:], wgs_second[:], wgs_rest[:, 0, :], wgs_rest[:, 1, :]]

        def put_columns(i, lo, hi, values):
            nc.vector.tensor_tensor(
                pages[i][:].indirect(list2[:, lo // 16 : hi // 16]), wgs_dealt[i % PACK][:, lo:hi], values, ALU.mult
            )

        def put_states(i):
            put_columns(i, 0, S, states[i][:])

        def put_piece(i, k):
            put_columns(i, *PIECES[i][k], states[i, k][:])

        first_bf = [held([P, WIDE, PACK], BF16, f"first_bf{c}") for c in range(T2 // WIDE)]
        first_c = {}
        first_s = [held([P, WIDE], U8, f"first_s{c}") for c in range(T2 // WIDE)]
        second_bf = [placed([P, UNIT, PACK], BF16, f"second_bf{c}", 2 * KIB * c) for c in range(UNITS)]
        second_c = [placed([P, UNIT], U32, f"second_c{c}", (16 + c) * KIB) for c in range(UNITS)]
        second_s = [placed([P, UNIT], U8, f"second_s{c}", 24 * KIB + UNIT * c) for c in range(UNITS)]

        def round_page(i, c):
            b, t = divmod(i, PACK)
            width = UNIT if b else WIDE
            target = second_bf[c] if b else first_bf[c]
            source = pages[i][:, c * width : (c + 1) * width]
            if i == TILES - 1 and c not in SCALAR_ROUND_UNITS:
                nc.vector.tensor_copy(out=target[:, :, t], in_=source)
            else:
                nc.scalar.copy(out=target[:, :, t], in_=source)

        def quantize_first(c):
            tag = ("least_late", f"state{TILES - 1}_1")[c]
            first_c[c] = keep.tile([P, WIDE], U32, name="first_c", tag=tag, align_bytes=64)
            nc.vector.quantize_mx(
                out=first_c[c][:].bitcast(E4M3), scales=first_s[c][:],
                in_=first_bf[c][:].rearrange("p c t -> p (c t)"),
            )

        def quantize_second(c):
            nc.vector.quantize_mx(
                out=second_c[c][:].bitcast(E4M3), scales=second_s[c][:],
                in_=second_bf[c][:].rearrange("p c t -> p (c t)"),
            )

        w2_w = held([P, 2, 2 * M], U8, "w2_w")
        w2_s = held([P, 2, M], U8, "w2_s")

        def deal_w2():
            for raw, dealt in ((w2_w_raw, w2_w), (w2_s_raw, w2_s)):
                nc.vector.tensor_copy(
                    out=dealt[:].bitcast(I32).rearrange("p a (t g e) -> p a t g e", t=PACK, g=16),
                    in_=raw[:].bitcast(I32).rearrange("p a (g t e) -> p a t g e", t=PACK, g=16),
                )

        w3_bf = held([P, N, PACK], BF16, "w3_bf")
        w3_codes = []
        w3_s = held([P, N], U8, "w3_s")

        def quantize_w3():
            w3_c = keep.tile([P, N], U32, name="w3_c", tag=f"state{TILES - 1}_0", align_bytes=64)
            w3_codes.append(w3_c)
            nc.vector.quantize_mx(
                out=w3_c[:].bitcast(E4M3), scales=w3_s[:], in_=w3_bf[:].rearrange("p n t -> p (n t)")
            )

        y_banks = {}

        def second_stage_pass(block, b):
            if b == 0:
                y_banks[block] = psum.tile([P, PACK, BANK_COLS], F32, name="y_bank", tag=f"y{block % Y_BANKS}")
            width = UNIT if b else WIDE
            c, start = divmod(block * BANK_COLS, width)
            codes, scales = (second_c[c], second_s[c]) if b else (first_c[c], first_s[c])
            for t in range(PACK):
                nc.tensor.matmul_mx(
                    out=y_banks[block][:, t, :],
                    lhsT=w2_w[:, b, 2 * t * P : 2 * (t + 1) * P].bitcast(E2M1),
                    lhsT_scale=w2_s[:, b, t * P : (t + 1) * P],
                    rhs=codes[:, start : start + BANK_COLS].bitcast(E4M3),
                    rhs_scale=scales[:, start : start + BANK_COLS],
                    start=(b == 0 and t == 0), stop=(b == 1 and t == PACK - 1),
                )

        quantize_w1(1)
        for i in range(PACK, TILES):
            make_states(i)
        nc.scalar.copy(out=w3_bf[:], in_=w3_raw[:].rearrange("p t n -> p n t"))

        one, other, least = {}, {}, {}

        def fetch_one(i):
            if i % 2 == 0 and i < TILES - 2:
                one[i] = keep.tile([P, PAIRS], F32, name="one", tag=f"state{i + 1}_0", align_bytes=64)
            else:
                one[i] = ring.tile([P, PAIRS], F32, name="one_odd", bufs=1)
            nc.vector.tensor_copy(out=one[i][:], in_=pages[i][:].indirect(list3[:]))

        def fetch_other(i):
            other[i] = ring.tile([P, PAIRS], F32, name="other")
            nc.vector.tensor_copy(out=other[i][:], in_=pages[i][:].indirect(list4[:]))

        def take_least(i):
            if i == TILES - 1:
                least[i] = keep.tile([P, PAIRS], F32, name="least_last", tag=f"page{i - 1}", align_bytes=64)
            elif i == TILES - 2:
                least[i] = keep.tile([P, PAIRS], F32, name="least_late", tag="least_late", align_bytes=64)
            else:
                least[i] = ring.tile([P, PAIRS], F32, name="least")
            nc.vector.tensor_tensor(least[i][:], one[i][:], other[i][:], ALU.min)

        def put_sum(i):
            nc.vector.tensor_tensor(pages[i][:].indirect(list3[:]), one[i][:], other[i][:], ALU.add)

        def put_least(i):
            nc.vector.tensor_copy(out=pages[i][:].indirect(list4[:]), in_=least[i][:])
            if i < TILES - 1:
                for c in range(T2 // WIDE if i < PACK else UNITS):
                    round_page(i, c)

        for k in range(len(PIECES[0])):
            put_piece(0, k)
        put_states(1)
        for a in range(0, TILES - 2, 2):
            for work in (fetch_one, fetch_other):
                work(a)
            for work in (fetch_one, fetch_other):
                work(a + 1)
            for work in (take_least, put_sum):
                work(a)
                work(a + 1)
            put_least(a)
            put_states(a + 2)
            if a + 3 < TILES - 1:
                put_states(a + 3)
            put_least(a + 1)
        a, b = TILES - 2, TILES - 1
        fetch_one(a)
        fetch_other(a)
        put_piece(b, 0)
        take_least(a)
        put_sum(a)
        put_piece(b, 1)
        put_least(a)
        fetch_one(b)
        fetch_other(b)
        deal_w2()
        quantize_w3()
        quantize_first(1)
        put_sum(b)
        take_least(b)
        quantize_first(0)
        for block in range(Y_BANKS):
            second_stage_pass(block, 0)
        put_least(b)

        blocks_per_unit = UNIT // BANK_COLS
        tanh_sb, z_bf, banks = {}, {}, {}
        out_rows = out.rearrange("(h p) c -> p h c", p=P)
        spans = [(c * UNIT, UNIT) for c in range(UNITS - 1)]
        spans = spans + [(T2 - UNIT, BANK_COLS), (T2 - BANK_COLS, BANK_COLS)]
        out_tags = ["side0", "side1"] * 3 + ["y4", "y5"]

        def second_stage(c):
            if c < TILES - 2:
                tanh_sb[c] = keep.tile([P, UNIT, PACK], F32, name="tanh_sb", tag=f"page{c}", align_bytes=64)
            else:
                tanh_sb[c] = placed([P, UNIT, PACK], F32, f"tanh_late{c}", (26 + 4 * (c - TILES + 2)) * KIB)
            for k in range(blocks_per_unit):
                block = c * blocks_per_unit + k
                if c >= EARLY_UNITS:
                    second_stage_pass(block, 0)
                second_stage_pass(block, 1)
                nc.scalar.activation(
                    out=tanh_sb[c][:, k * BANK_COLS : (k + 1) * BANK_COLS, :],
                    in_=y_banks[block][:].rearrange("p t c -> p c t"), func=ACT.Tanh,
                )

        def apply_gain2(k):
            start, width = spans[k]
            c, inner = divmod(start, UNIT)
            z_bf[k] = ring.tile([P, width, PACK], BF16, name="z_bf", align_bytes=64, bufs=3)
            nc.vector.tensor_tensor(
                z_bf[k][:], tanh_sb[c][:, inner : inner + width, :],
                gain2_sb[:].to_broadcast([P, width, PACK]), ALU.mult,
            )

        def third_stage(k):
            width = spans[k][1]
            z_c = ring.tile([P, width], U32, name="z_c", align_bytes=64)
            z_s = ring.tile([P, width], U8, name="z_s", align_bytes=64)
            nc.vector.quantize_mx(
                out=z_c[:].bitcast(E4M3), scales=z_s[:], in_=z_bf[k][:].rearrange("p c t -> p (c t)")
            )
            if k < len(out_tags):
                both = psum.tile([P, 2, width], F32, name="o_bank", tag=out_tags[k])
                banks[k] = [both[:, h, :] for h in range(2)]
            else:
                banks[k] = [psum.tile([P, width], F32, name="o_half", tag=f"y{h}")[:] for h in range(2)]
            for h in range(2):
                nc.tensor.matmul_mx(
                    out=banks[k][h],
                    lhsT=w3_codes[0][:, h * P : (h + 1) * P].bitcast(E4M3),
                    lhsT_scale=w3_s[:, h * P : (h + 1) * P],
                    rhs=z_c[:].bitcast(E4M3), rhs_scale=z_s[:],
                    start=True, stop=True,
                )

        def store(k):
            start, width = spans[k]
            result = placed([P, 2, width], F32, f"result{k}", (34 + 2 * k) * KIB)
            for h in range(2):
                if k == len(spans) - 1 and h == 1:
                    nc.vector.tensor_scalar(result[:, h, :], banks[k][h], b3_sb[:, h : h + 1], None, ALU.add)
                else:
                    nc.scalar.activation(
                        out=result[:, h, :], in_=banks[k][h], func=ACT.Identity, bias=b3_sb[:, h : h + 1]
                    )
            nc.sync.dma_start(out=out_rows[:, :, start : start + width], in_=result[:])

        round_lead, tanh_lead = 3, 4
        for step in range(UNITS + round_lead):
            if step < UNITS:
                round_page(TILES - 1, step)
            if step >= round_lead:
                quantize_second(step - round_lead)
                if step - round_lead < tanh_lead:
                    second_stage(step - round_lead)
        apply_gain2(0)
        for k in range(len(spans)):
            if k + 1 < len(spans):
                apply_gain2(k + 1)
            third_stage(k)
            store(k)
            if k + tanh_lead < UNITS:
                second_stage(k + tanh_lead)
